import numpy as np
import ml_dtypes


def mxq(x, axis, fmt="e4m3"):
    dtype, down = {"e4m3": (ml_dtypes.float8_e4m3fn, 7), "e5m2": (ml_dtypes.float8_e5m2, 14)}[fmt]
    v = np.moveaxis(np.asarray(x, np.float32).astype(ml_dtypes.bfloat16).astype(np.float64), axis, -1)
    blocks = v.reshape(v.shape[:-1] + (-1, 32))
    amax = np.abs(blocks).max(-1, keepdims=True)
    byte = np.maximum(np.where(amax > 0, np.frexp(amax)[1] - 1 + 127, 0) - down, 1)
    scale = np.exp2(byte - 127.0)
    codes = (blocks / scale).astype(np.float32).astype(dtype).astype(np.float64)
    return np.moveaxis((codes * scale).reshape(v.shape), -1, axis)


WIDE = False


def mx_kscale(k):
    if not WIDE:
        return np.ones(k)
    levels = np.array([10, -10, 5, -5, 0])
    if k % 512:
        return np.exp2(np.random.permutation(np.resize(levels, k // 32))).repeat(32)
    a = np.empty((k // 512, 16))
    for p in range(k // 512):
        a[p, :8] = np.random.permutation(np.resize(levels, 8))
        for g in range(8):
            far = levels[np.abs(levels - a[p, g]) >= 10]
            a[p, g + 8] = far[np.random.randint(len(far))]
    return np.exp2(a.ravel()).repeat(32)


def f64(x):
    return np.asarray(x).astype(np.float64)


def striped(idx):
    return np.tile(idx.reshape(-1, 16).T, (8, 1)).astype(np.uint16)


def unstriped(offs):
    return offs[:16].T.reshape(-1).astype(np.int64)


def striped8(idx):
    return np.concatenate([x.reshape(-1, 16).T for x in idx]).astype(np.uint16)


def runs(offs, k):
    lists = np.stack([offs[16 * r : 16 * r + 16].T.reshape(-1) for r in range(8)]).astype(np.int64)
    return lists[np.arange(k) % 512 // 64]


def pack_weight(w):
    k, n = w.shape
    w = f64(np.asarray(w, np.float32).astype(ml_dtypes.bfloat16)).reshape(k // 32, 32, n)
    amax = np.abs(w).max(1)
    byte = np.clip(np.where(amax > 0, np.frexp(amax)[1] - 1 + 127 - 7, 1), 1, 254)
    scaled = (w * np.exp2(127.0 - byte)[:, None, :]).reshape(k, n).astype(np.float32)
    words = np.ascontiguousarray(scaled.reshape(k // 512, 128, 4, n).transpose(0, 1, 3, 2)).astype(ml_dtypes.float8_e4m3fn).view(np.uint8)
    return words, np.ascontiguousarray(byte.astype(np.uint8).reshape(k // 512, 16, n))


def unpack_weight(words, scales):
    g, p, n, _ = words.shape
    vals = np.ascontiguousarray(words).view(ml_dtypes.float8_e4m3fn).astype(np.float64) * np.repeat(np.exp2(scales.astype(np.float64) - 127.0), 8, axis=1)[..., None]
    return vals.transpose(0, 1, 3, 2).reshape(g * 512, n)


def sigmoid(v):
    return 1.0 / (1.0 + np.exp(-np.maximum(v, -700.0)))


K, T, S, H, G, W = 512, 1024, 256, 512, 2048, 128


def setup_inputs():
    n = np.random.standard_normal
    s = mx_kscale(K)[:, None]
    packed_xT = pack_weight(n((K, T)) * s)
    packed_w1 = pack_weight(n((K, H)) / np.sqrt(2 * K) / s)
    packed_w2 = pack_weight(n((K, H)) / np.sqrt(2 * K) / s)
    packed_dT = pack_weight(n((K, G)) / s)
    perm = np.random.permutation(S)
    return {
        "x_words": packed_xT[0],
        "x_scales": packed_xT[1],
        "w1_words": packed_w1[0],
        "w1_scales": packed_w1[1],
        "w2_words": packed_w2[0],
        "w2_scales": packed_w2[1],
        "sl": np.random.uniform(1.0, 2.0, (H, 1)).astype(np.float32),
        "th": (0.5 * n((H, 1))).astype(np.float32),
        "gs": (np.random.uniform(0.5, 1.5, (K, 1)) * s).astype(np.float32),
        "d_words": packed_dT[0],
        "d_scales": packed_dT[1],
        "offs": striped(np.random.permutation(T)[:S]),
        "hz": striped8(np.random.randint(0, T, (8, S))),
        "n1": striped(np.random.permutation(S)),
        "n2": striped(np.random.permutation(S)),
        "n3": striped(np.random.permutation(S)),
        "k1": striped8(np.random.randint(0, G, (8, H))),
        "k2": striped8(np.random.randint(0, G, (8, H))),
        "two": striped(np.random.permutation(T)[:S]),
        "n4": striped(perm[:W]),
        "n5": striped(perm[W:]),
        "n6": striped(np.random.permutation(S)),
    }


def reference(x_words, x_scales, w1_words, w1_scales, w2_words, w2_scales, sl, th, gs, d_words, d_scales, offs, hz, n1, n2, n3, k1, k2, two, n4, n5, n6):
    d_k1 = unpack_weight(d_words, d_scales)[np.arange(K)[:, None], runs(k1, K)]
    xq = unpack_weight(x_words, x_scales)[:, unstriped(offs)]
    x_hz = unpack_weight(x_words, x_scales)[np.arange(K)[:, None], runs(hz, K)]
    y = unpack_weight(w1_words, w1_scales).T @ xq + unpack_weight(w2_words, w2_scales).T @ x_hz
    ds2 = np.zeros((H, S))
    ds2[:, unstriped(n2)] = y
    ds = np.zeros((H, S))
    ds[:, unstriped(n1)] = y
    sg = sigmoid(f64(sl) * (ds[:, unstriped(n3)] - f64(th)))
    z = f64(gs) * (ds2 * sg)
    d_k2 = unpack_weight(d_words, d_scales)[np.arange(K)[:, None], runs(k2, K)]
    x_two = unpack_weight(x_words, x_scales)[:, unstriped(two)]
    h2 = 0.0625 * ((d_k1.T @ mxq(z, 0, "e4m3") + d_k2.T @ x_two))
    pa = h2[:, unstriped(n4)]
    pb = h2[:, unstriped(n5)]
    rb = pa - pb
    ra = pa + pb
    ua = np.zeros((H, S))
    ua[:, unstriped(n4)] = ra
    ub = ua.copy()
    ub[:, unstriped(n5)] = rb
    return np.maximum(ub, ub[:, unstriped(n6)])

@@ -1,0 +1,244 @@
+from contextlib import ExitStack
+
+import concourse.mybir as mybir
+
+K, T, S, H, G, W = 512, 1024, 256, 512, 2048, 128
+FLOPS = 4 * 2 * K * H * S
+
+F32 = mybir.dt.float32
+BF16 = mybir.dt.bfloat16
+I32 = mybir.dt.int32
+U32 = mybir.dt.uint32
+U16 = mybir.dt.uint16
+U8 = mybir.dt.uint8
+FP8X4 = mybir.dt.float8_e4m3fn_x4
+ACT = mybir.ActivationFunctionType
+ALU = mybir.AluOpType
+
+P = 128
+PACK = 4
+TILES = H // P
+HALF = S // 2
+DS2_COLS = 352
+UB_COLS = 272
+Z_CHUNKS = ((0, 128), (128, 192), (192, 256))
+
+
+def entries(lst, a, b):
+    return lst[:, a // 16 : b // 16]
+
+
+def tile_picked_dthzmtesntwhaarh_none_p_kernel(
+    tc, x_words, x_scales, w1_words, w1_scales, w2_words, w2_scales, sl, th, gs, d_words, d_scales,
+    offs, hz, n1, n2, n3, k1, k2, two, n4, n5, n6, out,
+):
+    nc = tc.nc
+    with ExitStack() as ctx:
+        lists = ctx.enter_context(tc.tile_pool(name="lists", bufs=1))
+        keep = ctx.enter_context(tc.tile_pool(name="keep", bufs=1))
+        psum = ctx.enter_context(tc.psum_pool(name="psum", bufs=1))
+
+        def sbuf(name, shape, dtype, tag=""):
+            return keep.tile(shape, dtype, name=name, tag=tag, align_bytes=64)
+
+        def load_list(name, src):
+            tile = lists.tile(list(src.shape), U16, name=name)
+            nc.sync.dma_start(tile[:], src)
+            return tile
+
+        def load_words(queue, name, src, tag=""):
+            tile = sbuf(name, [P, src.shape[2]], U32, tag)
+            queue.dma_start(tile[:].bitcast(I32), src[0].rearrange("p c b -> p (c b)").bitcast(I32))
+            return tile
+
+        def load_scales(queue, dst, src):
+            rows = src[0].bitcast(I32)
+            queue.dma_start(dst.bitcast(I32), rows.unsqueeze(1).to_broadcast([16, 8, rows.shape[1]]))
+
+        def load_rows(queue, name, src):
+            tile = sbuf(name, [P, PACK], F32)
+            queue.dma_start(tile[:], src.rearrange("(p t) o -> p (t o)", t=PACK))
+            return tile
+
+        def gather(dst, window, offsets):
+            nc.vector.tensor_copy(dst, window[:].indirect(offsets))
+
+        def move_rows(queue, dst, src):
+            for r in (1, 2, 3):
+                queue.dma_start(dst[r:P:32, :].bitcast(I32), src[8 * r : P : 32, :].bitcast(I32))
+
+        def place_scales(name, picked):
+            placed = sbuf(name, list(picked.shape), U8)
+            nc.vector.tensor_copy(placed[:].bitcast(I32), picked[:].bitcast(I32))
+            move_rows(nc.sync, placed, picked)
+            return placed
+
+        def product(acc, lhs, lhs_s, rhs, rhs_s, first):
+            nc.tensor.matmul_mx(
+                out=acc, lhsT=lhs.bitcast(FP8X4), lhsT_scale=lhs_s, rhs=rhs.bitcast(FP8X4), rhs_scale=rhs_s,
+                start=first, stop=not first,
+            )
+
+        hz_l = load_list("hz_l", hz)
+        xs = sbuf("xs", [P, T], U8)
+        load_scales(nc.sync, xs[:], x_scales)
+        offs_l = load_list("offs_l", offs)
+        ws = sbuf("ws", [P, 2 * H], U8)
+        load_scales(nc.sync, ws[:, 0:H], w1_scales)
+        load_scales(nc.sync, ws[:, H : 2 * H], w2_scales)
+        n1_l = load_list("n1_l", n1)
+        n2_l = load_list("n2_l", n2)
+        xw = load_words(nc.sync, "xw", x_words)
+        w1w = load_words(nc.sync, "w1w", w1_words)
+        n3_l = load_list("n3_l", n3)
+        k1_l = load_list("k1_l", k1)
+        k2_l = load_list("k2_l", k2)
+        two_l = load_list("two_l", two)
+        n4_l = load_list("n4_l", n4)
+        n5_l = load_list("n5_l", n5)
+        w2w = load_words(nc.sync, "w2w", w2_words, "staged")
+        n6_l = load_list("n6_l", n6)
+        sl_t = load_rows(nc.gpsimd, "sl_t", sl)
+        th_t = load_rows(nc.gpsimd, "th_t", th)
+        gs_t = load_rows(nc.gpsimd, "gs_t", gs)
+        slth = sbuf("slth", [P, PACK], F32)
+        bias = sbuf("bias", [P, PACK], F32)
+        nc.gpsimd.tensor_tensor(slth[:], sl_t[:], th_t[:], ALU.mult)
+        nc.gpsimd.tensor_scalar(bias[:], slth[:], -1.0, 0.0, ALU.mult, ALU.add)
+
+        ub = [sbuf("ub%d" % t, [P, UB_COLS], F32) for t in range(TILES)]
+        for t in range(TILES):
+            nc.vector.memset(ub[t][:], 0.0)
+
+        x_b = sbuf("x_b", [P, 2 * S], U8, "bytes")
+        gather(x_b[:, 0:S], xs, hz_l[:])
+        gather(x_b[:, S : 2 * S], xs, offs_l[:])
+        x_s = place_scales("x_s", x_b)
+        hz_s = x_s[:, 0:S]
+        xq_s = x_s[:, S : 2 * S]
+
+        wsd = sbuf("wsd", [P, 2, TILES, P], U8)
+        nc.vector.tensor_copy(wsd[:], ws[:].rearrange("p (a m t) -> p a t m", a=2, t=PACK))
+        w1d = sbuf("w1d", [P, TILES, P], U32)
+        w2d = sbuf("w2d", [P, TILES, P], U32)
+        nc.scalar.copy(w1d[:].rearrange("p t m -> p m t"), w1w[:].rearrange("p (m t) -> p m t", t=PACK))
+        wsd_rows = wsd[:].rearrange("p a t m -> p (a t m)")
+        move_rows(nc.scalar, wsd_rows, wsd_rows)
+        nc.scalar.copy(w2d[:].rearrange("p t m -> p m t"), w2w[:].rearrange("p (m t) -> p m t", t=PACK))
+
+        xq_w = sbuf("xq_w", [P, S], U32)
+        hz_w = sbuf("hz_w", [P, S], U32)
+        gather(xq_w[:], xw, offs_l[:])
+        gather(hz_w[:], xw, hz_l[:])
+
+        y = [sbuf("y%d" % t, [P, S], F32) for t in range(TILES)]
+        pieces = [(0, 0, HALF), (0, HALF, S)] + [(t, 0, S) for t in range(1, TILES)]
+        for bank, (t, a, b) in enumerate(pieces):
+            acc = psum.tile([P, b - a], F32, name="y_acc%d" % bank, tag="bank%d" % bank)
+            product(acc[:], w1d[:, t, :], wsd[:, 0, t, :], xq_w[:, a:b], xq_s[:, a:b], True)
+            product(acc[:], w2d[:, t, :], wsd[:, 1, t, :], hz_w[:, a:b], hz_s[:, a:b], False)
+            if bank == 0:
+                nc.scalar.copy(y[t][:, a:b], acc[:])
+            else:
+                nc.vector.tensor_copy(y[t][:, a:b], acc[:])
+
+        dsc = sbuf("dsc", [P, G], U8, "bytes")
+        load_scales(nc.sync, dsc[:], d_scales)
+        dw = load_words(nc.sync, "dw", d_words, "staged")
+
+        ds = [sbuf("ds%d" % t, [P, S], F32) for t in range(TILES)]
+        ds2 = [sbuf("ds2_%d" % t, [P, DS2_COLS], F32) for t in range(TILES)]
+
+        def scatter(window, offsets, values):
+            nc.scalar.activation(window[:].indirect(offsets), values, ACT.Copy)
+
+        def fetch(dst, window, offsets):
+            nc.scalar.activation(dst, window[:].indirect(offsets), ACT.Copy)
+
+        code_b = sbuf("code_b", [P, 2 * H + S], U8)
+        two_w = sbuf("two_w", [P, S], U32)
+        d1_w = sbuf("d1_w", [P, H], U32)
+        d2_w = sbuf("d2_w", [P, H], U32)
+        gather(code_b[:, 0:H], dsc, k1_l[:])
+        gather(code_b[:, H : 2 * H], dsc, k2_l[:])
+        gather(code_b[:, 2 * H : 2 * H + S], xs, two_l[:])
+        code_s = place_scales("code_s", code_b)
+        two_s = code_s[:, 2 * H : 2 * H + S]
+        gather(two_w[:], xw, two_l[:])
+        gather(d2_w[:], dw, k2_l[:])
+        gather(d1_w[:], dw, k1_l[:])
+        ds2g = sbuf("ds2g", [P, S, PACK], F32, "staged")
+
+        for t in range(TILES):
+            scatter(ds[t], entries(n1_l, 0, HALF), y[t][:, 0:HALF])
+            scatter(ds2[t], n2_l[:], y[t][:])
+            scatter(ds[t], entries(n1_l, HALF, S), y[t][:, HALF:S])
+            nc.vector.tensor_scalar(ds2g[:, :, t], ds2[t][:, 0:S], gs_t[:, t : t + 1], None, ALU.mult)
+
+        h_pieces = [(0, 0, HALF, 5), (0, HALF, S, 6), (1, 0, S, 7), (2, 0, S, 0), (3, 0, S, 1)]
+        h_acc = []
+        for t, a, b, bank in h_pieces:
+            acc = psum.tile([P, b - a], F32, name="h_acc%d" % bank, tag="bank%d" % bank)
+            cols = slice(t * P, (t + 1) * P)
+            product(acc[:], d2_w[:, cols], code_s[:, H + t * P : H + (t + 1) * P], two_w[:, a:b], two_s[:, a:b], True)
+            h_acc.append(acc)
+
+        z_w = sbuf("z_w", [P, S], U32)
+        z_s = sbuf("z_s", [P, S], U8)
+        h2 = [sbuf("h2_%d" % t, [P, S], F32) for t in range(TILES)]
+
+        def close(i):
+            t, a, b, bank = h_pieces[i]
+            cols = slice(t * P, (t + 1) * P)
+            product(h_acc[i][:], d1_w[:, cols], code_s[:, cols], z_w[:, a:b], z_s[:, a:b], False)
+            if i == 1:
+                nc.scalar.activation(h2[t][:, a:b], h_acc[i][:], ACT.Copy, scale=0.0625)
+            else:
+                nc.vector.tensor_scalar(h2[t][:, a:b], h_acc[i][:], 0.0625, None, ALU.mult)
+
+        for c, (a, b) in enumerate(Z_CHUNKS):
+            sg = sbuf("sg%d" % c, [P, PACK, b - a], F32)
+            for t in range(TILES):
+                nc.scalar.activation(
+                    sg[:, t, :], ds[t][:].indirect(entries(n3_l, a, b)), ACT.Sigmoid,
+                    bias=bias[:, t : t + 1], scale=sl_t[:, t : t + 1],
+                )
+            zb = sbuf("zb%d" % c, [P, b - a, PACK], BF16)
+            nc.vector.tensor_tensor(zb[:], ds2g[:, a:b, :], sg[:].rearrange("p t j -> p j t"), ALU.mult)
+            nc.vector.quantize_mx(
+                out=z_w[:, a:b].bitcast(FP8X4), scales=z_s[:, a:b], in_=zb[:].rearrange("p j t -> p (j t)")
+            )
+            if c == 0:
+                close(0)
+        for i in range(1, len(h_pieces)):
+            close(i)
+
+        pa = [sbuf("pa%d" % t, [P, W], F32) for t in range(TILES)]
+        pb = [sbuf("pb%d" % t, [P, W], F32) for t in range(TILES)]
+        ra = [sbuf("ra%d" % t, [P, W], F32) for t in range(TILES)]
+        rb = [sbuf("rb%d" % t, [P, W], F32) for t in range(TILES)]
+        far = [sbuf("far%d" % t, [P, S], F32) for t in range(TILES)]
+        res = [sbuf("res%d" % t, [P, S], F32) for t in range(TILES)]
+
+        def pair(t):
+            fetch(pa[t][:], h2[t], n4_l[:])
+            fetch(pb[t][:], h2[t], n5_l[:])
+            nc.vector.tensor_tensor(ra[t][:], pa[t][:], pb[t][:], ALU.add)
+            nc.vector.tensor_tensor(rb[t][:], pa[t][:], pb[t][:], ALU.subtract)
+
+        def finish(t, a, b):
+            fetch(far[t][:, a:b], ub[t], entries(n6_l, a, b))
+            nc.vector.tensor_tensor(res[t][:, a:b], ub[t][:, a:b], far[t][:, a:b], ALU.max)
+            nc.sync.dma_start(out[t * P : (t + 1) * P, a:b], res[t][:, a:b])
+
+        pair(0)
+        pair(1)
+        for t in range(TILES):
+            scatter(ub[t], n4_l[:], ra[t][:])
+            if t > 0:
+                finish(t - 1, 0, S)
+            if t + 2 < TILES:
+                pair(t + 2)
+            scatter(ub[t], n5_l[:], rb[t][:])
+        finish(TILES - 1, 0, HALF)
+        finish(TILES - 1, HALF, S)

@@ -106,6 +106,11 @@ def tile_picked_dthzmtesntwhaarh_none_p_kernel(
         nc.gpsimd.tensor_tensor(slth[:], sl_t[:], th_t[:], ALU.mult)
         nc.gpsimd.tensor_scalar(bias[:], slth[:], -1.0, 0.0, ALU.mult, ALU.add)
 
+        warm_in = sbuf("warm_in", [P, 1], F32)
+        warm_out = sbuf("warm_out", [P, 1], F32)
+        nc.vector.memset(warm_in[:], 0.0)
+        nc.scalar.activation(warm_out[:], warm_in[:], ACT.Sigmoid)
+
         ub = [sbuf("ub%d" % t, [P, UB_COLS], F32) for t in range(TILES)]
         for t in range(TILES):
             nc.vector.memset(ub[t][:], 0.0)

@@ -21,7 +21,8 @@ TILES = H // P
 HALF = S // 2
 DS2_COLS = 352
 UB_COLS = 272
-Z_CHUNKS = ((0, 128), (128, 192), (192, 256))
+Z_CHUNKS = ((0, 128), (128, 256))
+DS_COLS = 384
 
 
 def entries(lst, a, b):
@@ -81,30 +82,16 @@ def tile_picked_dthzmtesntwhaarh_none_p_kernel(
 
         hz_l = load_list("hz_l", hz)
         xs = sbuf("xs", [P, T], U8)
-        load_scales(nc.sync, xs[:], x_scales)
+        load_scales(nc.scalar, xs[:], x_scales)
         offs_l = load_list("offs_l", offs)
         ws = sbuf("ws", [P, 2 * H], U8)
-        load_scales(nc.sync, ws[:, 0:H], w1_scales)
-        load_scales(nc.sync, ws[:, H : 2 * H], w2_scales)
+        load_scales(nc.scalar, ws[:, 0:H], w1_scales)
+        load_scales(nc.scalar, ws[:, H : 2 * H], w2_scales)
         n1_l = load_list("n1_l", n1)
-        n2_l = load_list("n2_l", n2)
         xw = load_words(nc.sync, "xw", x_words)
         w1w = load_words(nc.sync, "w1w", w1_words)
-        n3_l = load_list("n3_l", n3)
-        k1_l = load_list("k1_l", k1)
-        k2_l = load_list("k2_l", k2)
-        two_l = load_list("two_l", two)
-        n4_l = load_list("n4_l", n4)
-        n5_l = load_list("n5_l", n5)
         w2w = load_words(nc.sync, "w2w", w2_words, "staged")
-        n6_l = load_list("n6_l", n6)
-        sl_t = load_rows(nc.gpsimd, "sl_t", sl)
-        th_t = load_rows(nc.gpsimd, "th_t", th)
-        gs_t = load_rows(nc.gpsimd, "gs_t", gs)
-        slth = sbuf("slth", [P, PACK], F32)
-        bias = sbuf("bias", [P, PACK], F32)
-        nc.gpsimd.tensor_tensor(slth[:], sl_t[:], th_t[:], ALU.mult)
-        nc.gpsimd.tensor_scalar(bias[:], slth[:], -1.0, 0.0, ALU.mult, ALU.add)
+        move_rows(nc.scalar, ws, ws)
 
         warm_in = sbuf("warm_in", [P, 1], F32)
         warm_out = sbuf("warm_out", [P, 1], F32)
@@ -122,14 +109,30 @@ def tile_picked_dthzmtesntwhaarh_none_p_kernel(
         hz_s = x_s[:, 0:S]
         xq_s = x_s[:, S : 2 * S]
 
-        wsd = sbuf("wsd", [P, 2, TILES, P], U8)
-        nc.vector.tensor_copy(wsd[:], ws[:].rearrange("p (a m t) -> p a t m", a=2, t=PACK))
+        n2_l = load_list("n2_l", n2)
+        two_l = load_list("two_l", two)
+        n3_l = load_list("n3_l", n3)
+        k1_l = load_list("k1_l", k1)
+        k2_l = load_list("k2_l", k2)
+        n4_l = load_list("n4_l", n4)
+        n5_l = load_list("n5_l", n5)
+        n6_l = load_list("n6_l", n6)
+        sl_t = load_rows(nc.sync, "sl_t", sl)
+        th_t = load_rows(nc.sync, "th_t", th)
+        gs_t = load_rows(nc.sync, "gs_t", gs)
+
         w1d = sbuf("w1d", [P, TILES, P], U32)
         w2d = sbuf("w2d", [P, TILES, P], U32)
         nc.scalar.copy(w1d[:].rearrange("p t m -> p m t"), w1w[:].rearrange("p (m t) -> p m t", t=PACK))
-        wsd_rows = wsd[:].rearrange("p a t m -> p (a t m)")
-        move_rows(nc.scalar, wsd_rows, wsd_rows)
         nc.scalar.copy(w2d[:].rearrange("p t m -> p m t"), w2w[:].rearrange("p (m t) -> p m t", t=PACK))
+        ws_view = ws[:].rearrange("p (a m t) -> p a t m", a=2, t=PACK)
+        wsd0 = sbuf("wsd0", [P, 2, 1, P], U8)
+        wsd1 = sbuf("wsd1", [P, 2, TILES - 1, P], U8)
+        nc.vector.tensor_copy(wsd0[:], ws_view[:, :, 0:1, :])
+        nc.vector.tensor_copy(wsd1[:], ws_view[:, :, 1:TILES, :])
+
+        def w_scale(a, t):
+            return wsd0[:, a, 0, :] if t == 0 else wsd1[:, a, t - 1, :]
 
         xq_w = sbuf("xq_w", [P, S], U32)
         hz_w = sbuf("hz_w", [P, S], U32)
@@ -140,8 +143,8 @@ def tile_picked_dthzmtesntwhaarh_none_p_kernel(
         pieces = [(0, 0, HALF), (0, HALF, S)] + [(t, 0, S) for t in range(1, TILES)]
         for bank, (t, a, b) in enumerate(pieces):
             acc = psum.tile([P, b - a], F32, name="y_acc%d" % bank, tag="bank%d" % bank)
-            product(acc[:], w1d[:, t, :], wsd[:, 0, t, :], xq_w[:, a:b], xq_s[:, a:b], True)
-            product(acc[:], w2d[:, t, :], wsd[:, 1, t, :], hz_w[:, a:b], hz_s[:, a:b], False)
+            product(acc[:], w1d[:, t, :], w_scale(0, t), xq_w[:, a:b], xq_s[:, a:b], True)
+            product(acc[:], w2d[:, t, :], w_scale(1, t), hz_w[:, a:b], hz_s[:, a:b], False)
             if bank == 0:
                 nc.scalar.copy(y[t][:, a:b], acc[:])
             else:
@@ -151,7 +154,7 @@ def tile_picked_dthzmtesntwhaarh_none_p_kernel(
         load_scales(nc.sync, dsc[:], d_scales)
         dw = load_words(nc.sync, "dw", d_words, "staged")
 
-        ds = [sbuf("ds%d" % t, [P, S], F32) for t in range(TILES)]
+        ds = [sbuf("ds%d" % t, [P, DS_COLS], F32) for t in range(TILES)]
         ds2 = [sbuf("ds2_%d" % t, [P, DS2_COLS], F32) for t in range(TILES)]
 
         def scatter(window, offsets, values):
@@ -173,11 +176,17 @@ def tile_picked_dthzmtesntwhaarh_none_p_kernel(
         gather(d2_w[:], dw, k2_l[:])
         gather(d1_w[:], dw, k1_l[:])
         ds2g = sbuf("ds2g", [P, S, PACK], F32, "staged")
+        bias = sbuf("bias", [P, PACK], F32)
+        nc.vector.scalar_tensor_tensor(bias[:], sl_t[:], -1.0, th_t[:], ALU.mult, ALU.mult)
 
         for t in range(TILES):
-            scatter(ds[t], entries(n1_l, 0, HALF), y[t][:, 0:HALF])
-            scatter(ds2[t], n2_l[:], y[t][:])
-            scatter(ds[t], entries(n1_l, HALF, S), y[t][:, HALF:S])
+            if t == 0:
+                scatter(ds[t], entries(n1_l, 0, HALF), y[t][:, 0:HALF])
+                scatter(ds2[t], n2_l[:], y[t][:])
+                scatter(ds[t], entries(n1_l, HALF, S), y[t][:, HALF:S])
+            else:
+                scatter(ds2[t], n2_l[:], y[t][:])
+                scatter(ds[t], n1_l[:], y[t][:])
             nc.vector.tensor_scalar(ds2g[:, :, t], ds2[t][:, 0:S], gs_t[:, t : t + 1], None, ALU.mult)
 
         h_pieces = [(0, 0, HALF, 5), (0, HALF, S, 6), (1, 0, S, 7), (2, 0, S, 0), (3, 0, S, 1)]
@@ -202,14 +211,17 @@ def tile_picked_dthzmtesntwhaarh_none_p_kernel(
                 nc.vector.tensor_scalar(h2[t][:, a:b], h_acc[i][:], 0.0625, None, ALU.mult)
 
         for c, (a, b) in enumerate(Z_CHUNKS):
-            sg = sbuf("sg%d" % c, [P, PACK, b - a], F32)
-            for t in range(TILES):
-                nc.scalar.activation(
-                    sg[:, t, :], ds[t][:].indirect(entries(n3_l, a, b)), ACT.Sigmoid,
-                    bias=bias[:, t : t + 1], scale=sl_t[:, t : t + 1],
-                )
             zb = sbuf("zb%d" % c, [P, b - a, PACK], BF16)
-            nc.vector.tensor_tensor(zb[:], ds2g[:, a:b, :], sg[:].rearrange("p t j -> p j t"), ALU.mult)
+            for t0 in (0, 2):
+                sg = sbuf("sg%d_%d" % (c, t0), [P, 2, b - a], F32)
+                for t in (t0, t0 + 1):
+                    nc.scalar.activation(
+                        sg[:, t - t0, :], ds[t][:].indirect(entries(n3_l, a, b)), ACT.Sigmoid,
+                        bias=bias[:, t : t + 1], scale=sl_t[:, t : t + 1],
+                    )
+                nc.vector.tensor_tensor(
+                    zb[:, :, t0 : t0 + 2], ds2g[:, a:b, t0 : t0 + 2], sg[:].rearrange("p t j -> p j t"), ALU.mult
+                )
             nc.vector.quantize_mx(
                 out=z_w[:, a:b].bitcast(FP8X4), scales=z_s[:, a:b], in_=zb[:].rearrange("p j t -> p (j t)")
             )
@@ -245,5 +257,5 @@ def tile_picked_dthzmtesntwhaarh_none_p_kernel(
             if t + 2 < TILES:
                 pair(t + 2)
             scatter(ub[t], n5_l[:], rb[t][:])
-        finish(TILES - 1, 0, HALF)
-        finish(TILES - 1, HALF, S)
+        finish(TILES - 1, 0, S - 64)
+        finish(TILES - 1, S - 64, S)

@@ -64,15 +64,13 @@ def tile_picked_dthzmtesntwhaarh_none_p_kernel(
         def gather(dst, window, offsets):
             nc.vector.tensor_copy(dst, window[:].indirect(offsets))
 
-        def move_rows(queue, dst, src):
-            for r in (1, 2, 3):
-                queue.dma_start(dst[r:P:32, :].bitcast(I32), src[8 * r : P : 32, :].bitcast(I32))
+        def move_row(queue, dst, src, r):
+            queue.dma_start(dst[r:P:32, :].bitcast(I32), src[8 * r : P : 32, :].bitcast(I32))
 
-        def place_scales(name, picked):
-            placed = sbuf(name, list(picked.shape), U8)
-            nc.vector.tensor_copy(placed[:].bitcast(I32), picked[:].bitcast(I32))
-            move_rows(nc.sync, placed, picked)
-            return placed
+        def cleared(name, cols):
+            tile = sbuf(name, [P, cols], U8)
+            nc.vector.memset(tile[:].bitcast(I32), 0)
+            return tile
 
         def product(acc, lhs, lhs_s, rhs, rhs_s, first):
             nc.tensor.matmul_mx(
@@ -84,28 +82,33 @@ def tile_picked_dthzmtesntwhaarh_none_p_kernel(
         xs = sbuf("xs", [P, T], U8)
         load_scales(nc.scalar, xs[:], x_scales)
         offs_l = load_list("offs_l", offs)
-        ws = sbuf("ws", [P, 2 * H], U8)
+        ws = sbuf("ws", [P, 2 * H], U8, "bytes")
         load_scales(nc.scalar, ws[:, 0:H], w1_scales)
         load_scales(nc.scalar, ws[:, H : 2 * H], w2_scales)
         n1_l = load_list("n1_l", n1)
         xw = load_words(nc.sync, "xw", x_words)
         w1w = load_words(nc.sync, "w1w", w1_words)
-        w2w = load_words(nc.sync, "w2w", w2_words, "staged")
-        move_rows(nc.scalar, ws, ws)
+        w2w = load_words(nc.sync, "w2w", w2_words)
+        for r in (1, 2, 3):
+            move_row(nc.sync, ws, ws, r)
 
         warm_in = sbuf("warm_in", [P, 1], F32)
         warm_out = sbuf("warm_out", [P, 1], F32)
         nc.vector.memset(warm_in[:], 0.0)
         nc.scalar.activation(warm_out[:], warm_in[:], ACT.Sigmoid)
 
+        code_s = cleared("code_s", 2 * H + S)
         ub = [sbuf("ub%d" % t, [P, UB_COLS], F32) for t in range(TILES)]
         for t in range(TILES):
             nc.vector.memset(ub[t][:], 0.0)
 
-        x_b = sbuf("x_b", [P, 2 * S], U8, "bytes")
+        x_b = sbuf("x_b", [P, 2 * S], U8, "staged")
         gather(x_b[:, 0:S], xs, hz_l[:])
         gather(x_b[:, S : 2 * S], xs, offs_l[:])
-        x_s = place_scales("x_s", x_b)
+        x_s = sbuf("x_s", [P, 2 * S], U8)
+        nc.vector.tensor_copy(x_s[:].bitcast(I32), x_b[:].bitcast(I32))
+        for r in (1, 2, 3):
+            move_row(nc.sync if r == 3 else nc.scalar, x_s, x_b, r)
         hz_s = x_s[:, 0:S]
         xq_s = x_s[:, S : 2 * S]
 
@@ -123,8 +126,10 @@ def tile_picked_dthzmtesntwhaarh_none_p_kernel(
 
         w1d = sbuf("w1d", [P, TILES, P], U32)
         w2d = sbuf("w2d", [P, TILES, P], U32)
-        nc.scalar.copy(w1d[:].rearrange("p t m -> p m t"), w1w[:].rearrange("p (m t) -> p m t", t=PACK))
-        nc.scalar.copy(w2d[:].rearrange("p t m -> p m t"), w2w[:].rearrange("p (m t) -> p m t", t=PACK))
+        for dealt, raw in ((w1d, w1w), (w2d, w2w)):
+            nc.scalar.copy(
+                dealt[:].rearrange("p t (c i) -> p c t i", i=4), raw[:].rearrange("p (c i t) -> p c t i", i=4, t=PACK)
+            )
         ws_view = ws[:].rearrange("p (a m t) -> p a t m", a=2, t=PACK)
         wsd0 = sbuf("wsd0", [P, 2, 1, P], U8)
         wsd1 = sbuf("wsd1", [P, 2, TILES - 1, P], U8)
@@ -170,7 +175,8 @@ def tile_picked_dthzmtesntwhaarh_none_p_kernel(
         gather(code_b[:, 0:H], dsc, k1_l[:])
         gather(code_b[:, H : 2 * H], dsc, k2_l[:])
         gather(code_b[:, 2 * H : 2 * H + S], xs, two_l[:])
-        code_s = place_scales("code_s", code_b)
+        for r in range(4):
+            move_row(nc.sync, code_s, code_b, r)
         two_s = code_s[:, 2 * H : 2 * H + S]
         gather(two_w[:], xw, two_l[:])
         gather(d2_w[:], dw, k2_l[:])
@@ -248,14 +254,20 @@ def tile_picked_dthzmtesntwhaarh_none_p_kernel(
             nc.vector.tensor_tensor(res[t][:, a:b], ub[t][:, a:b], far[t][:, a:b], ALU.max)
             nc.sync.dma_start(out[t * P : (t + 1) * P, a:b], res[t][:, a:b])
 
+        def put_back(tiles):
+            for t in tiles:
+                scatter(ub[t], n4_l[:], ra[t][:])
+            for t in tiles:
+                scatter(ub[t], n5_l[:], rb[t][:])
+
         pair(0)
         pair(1)
-        for t in range(TILES):
-            scatter(ub[t], n4_l[:], ra[t][:])
-            if t > 0:
-                finish(t - 1, 0, S)
-            if t + 2 < TILES:
-                pair(t + 2)
-            scatter(ub[t], n5_l[:], rb[t][:])
-        finish(TILES - 1, 0, S - 64)
-        finish(TILES - 1, S - 64, S)
+        put_back((0, 1))
+        pair(2)
+        pair(3)
+        finish(0, 0, S)
+        finish(1, 0, S)
+        put_back((2, 3))
+        finish(2, 0, S)
+        finish(3, 0, S - 64)
+        finish(3, S - 64, S)

from contextlib import ExitStack

import concourse.mybir as mybir

K, T, S, H, G, W = 512, 1024, 256, 512, 2048, 128
FLOPS = 4 * 2 * K * H * S

F32 = mybir.dt.float32
BF16 = mybir.dt.bfloat16
I32 = mybir.dt.int32
U32 = mybir.dt.uint32
U16 = mybir.dt.uint16
U8 = mybir.dt.uint8
FP8X4 = mybir.dt.float8_e4m3fn_x4
ACT = mybir.ActivationFunctionType
ALU = mybir.AluOpType

P = 128
PACK = 4
TILES = H // P
HALF = S // 2
DS2_COLS = 352
UB_COLS = 272
Z_CHUNKS = ((0, 128), (128, 256))
DS_COLS = 384


def entries(lst, a, b):
    return lst[:, a // 16 : b // 16]


def tile_picked_dthzmtesntwhaarh_none_p_kernel(
    tc, x_words, x_scales, w1_words, w1_scales, w2_words, w2_scales, sl, th, gs, d_words, d_scales,
    offs, hz, n1, n2, n3, k1, k2, two, n4, n5, n6, out,
):
    nc = tc.nc
    with ExitStack() as ctx:
        lists = ctx.enter_context(tc.tile_pool(name="lists", bufs=1))
        keep = ctx.enter_context(tc.tile_pool(name="keep", bufs=1))
        psum = ctx.enter_context(tc.psum_pool(name="psum", bufs=1))

        def sbuf(name, shape, dtype, tag=""):
            return keep.tile(shape, dtype, name=name, tag=tag, align_bytes=64)

        def load_list(name, src):
            tile = lists.tile(list(src.shape), U16, name=name)
            nc.sync.dma_start(tile[:], src)
            return tile

        def load_words(queue, name, src, tag=""):
            tile = sbuf(name, [P, src.shape[2]], U32, tag)
            queue.dma_start(tile[:].bitcast(I32), src[0].rearrange("p c b -> p (c b)").bitcast(I32))
            return tile

        def load_scales(queue, dst, src):
            rows = src[0].bitcast(I32)
            queue.dma_start(dst.bitcast(I32), rows.unsqueeze(1).to_broadcast([16, 8, rows.shape[1]]))

        def load_rows(queue, name, src):
            tile = sbuf(name, [P, PACK], F32)
            queue.dma_start(tile[:], src.rearrange("(p t) o -> p (t o)", t=PACK))
            return tile

        def gather(dst, window, offsets):
            nc.vector.tensor_copy(dst, window[:].indirect(offsets))

        def move_row(queue, dst, src, r):
            queue.dma_start(dst[r:P:32, :].bitcast(I32), src[8 * r : P : 32, :].bitcast(I32))

        def cleared(name, cols):
            tile = sbuf(name, [P, cols], U8)
            nc.vector.memset(tile[:].bitcast(I32), 0)
            return tile

        def product(acc, lhs, lhs_s, rhs, rhs_s, first):
            nc.tensor.matmul_mx(
                out=acc, lhsT=lhs.bitcast(FP8X4), lhsT_scale=lhs_s, rhs=rhs.bitcast(FP8X4), rhs_scale=rhs_s,
                start=first, stop=not first,
            )

        hz_l = load_list("hz_l", hz)
        xs = sbuf("xs", [P, T], U8)
        load_scales(nc.scalar, xs[:], x_scales)
        offs_l = load_list("offs_l", offs)
        ws = sbuf("ws", [P, 2 * H], U8, "bytes")
        load_scales(nc.scalar, ws[:, 0:H], w1_scales)
        load_scales(nc.scalar, ws[:, H : 2 * H], w2_scales)
        n1_l = load_list("n1_l", n1)
        xw = load_words(nc.sync, "xw", x_words)
        w1w = load_words(nc.sync, "w1w", w1_words)
        w2w = load_words(nc.sync, "w2w", w2_words)
        for r in (1, 2, 3):
            move_row(nc.sync, ws, ws, r)

        warm_in = sbuf("warm_in", [P, 1], F32)
        warm_out = sbuf("warm_out", [P, 1], F32)
        nc.vector.memset(warm_in[:], 0.0)
        nc.scalar.activation(warm_out[:], warm_in[:], ACT.Sigmoid)

        code_s = cleared("code_s", 2 * H + S)
        ub = [sbuf("ub%d" % t, [P, UB_COLS], F32) for t in range(TILES)]
        for t in range(TILES):
            nc.vector.memset(ub[t][:], 0.0)

        x_b = sbuf("x_b", [P, 2 * S], U8, "staged")
        gather(x_b[:, 0:S], xs, hz_l[:])
        gather(x_b[:, S : 2 * S], xs, offs_l[:])
        x_s = sbuf("x_s", [P, 2 * S], U8)
        nc.vector.tensor_copy(x_s[:].bitcast(I32), x_b[:].bitcast(I32))
        for r in (1, 2, 3):
            move_row(nc.sync if r == 3 else nc.scalar, x_s, x_b, r)
        hz_s = x_s[:, 0:S]
        xq_s = x_s[:, S : 2 * S]

        n2_l = load_list("n2_l", n2)
        two_l = load_list("two_l", two)
        n3_l = load_list("n3_l", n3)
        k1_l = load_list("k1_l", k1)
        k2_l = load_list("k2_l", k2)
        n4_l = load_list("n4_l", n4)
        n5_l = load_list("n5_l", n5)
        n6_l = load_list("n6_l", n6)
        sl_t = load_rows(nc.sync, "sl_t", sl)
        th_t = load_rows(nc.sync, "th_t", th)
        gs_t = load_rows(nc.sync, "gs_t", gs)

        w1d = sbuf("w1d", [P, TILES, P], U32)
        w2d = sbuf("w2d", [P, TILES, P], U32)
        for dealt, raw in ((w1d, w1w), (w2d, w2w)):
            nc.scalar.copy(
                dealt[:].rearrange("p t (c i) -> p c t i", i=4), raw[:].rearrange("p (c i t) -> p c t i", i=4, t=PACK)
            )
        ws_view = ws[:].rearrange("p (a m t) -> p a t m", a=2, t=PACK)
        wsd0 = sbuf("wsd0", [P, 2, 1, P], U8)
        wsd1 = sbuf("wsd1", [P, 2, TILES - 1, P], U8)
        nc.vector.tensor_copy(wsd0[:], ws_view[:, :, 0:1, :])
        nc.vector.tensor_copy(wsd1[:], ws_view[:, :, 1:TILES, :])

        def w_scale(a, t):
            return wsd0[:, a, 0, :] if t == 0 else wsd1[:, a, t - 1, :]

        xq_w = sbuf("xq_w", [P, S], U32)
        hz_w = sbuf("hz_w", [P, S], U32)
        gather(xq_w[:], xw, offs_l[:])
        gather(hz_w[:], xw, hz_l[:])

        y = [sbuf("y%d" % t, [P, S], F32) for t in range(TILES)]
        pieces = [(0, 0, HALF), (0, HALF, S)] + [(t, 0, S) for t in range(1, TILES)]
        for bank, (t, a, b) in enumerate(pieces):
            acc = psum.tile([P, b - a], F32, name="y_acc%d" % bank, tag="bank%d" % bank)
            product(acc[:], w1d[:, t, :], w_scale(0, t), xq_w[:, a:b], xq_s[:, a:b], True)
            product(acc[:], w2d[:, t, :], w_scale(1, t), hz_w[:, a:b], hz_s[:, a:b], False)
            if bank == 0:
                nc.scalar.copy(y[t][:, a:b], acc[:])
            else:
                nc.vector.tensor_copy(y[t][:, a:b], acc[:])

        dsc = sbuf("dsc", [P, G], U8, "bytes")
        load_scales(nc.sync, dsc[:], d_scales)
        dw = load_words(nc.sync, "dw", d_words, "staged")

        ds = [sbuf("ds%d" % t, [P, DS_COLS], F32) for t in range(TILES)]
        ds2 = [sbuf("ds2_%d" % t, [P, DS2_COLS], F32) for t in range(TILES)]

        def scatter(window, offsets, values):
            nc.scalar.activation(window[:].indirect(offsets), values, ACT.Copy)

        def fetch(dst, window, offsets):
            nc.scalar.activation(dst, window[:].indirect(offsets), ACT.Copy)

        code_b = sbuf("code_b", [P, 2 * H + S], U8)
        two_w = sbuf("two_w", [P, S], U32)
        d1_w = sbuf("d1_w", [P, H], U32)
        d2_w = sbuf("d2_w", [P, H], U32)
        gather(code_b[:, 0:H], dsc, k1_l[:])
        gather(code_b[:, H : 2 * H], dsc, k2_l[:])
        gather(code_b[:, 2 * H : 2 * H + S], xs, two_l[:])
        for r in range(4):
            move_row(nc.sync, code_s, code_b, r)
        two_s = code_s[:, 2 * H : 2 * H + S]
        gather(two_w[:], xw, two_l[:])
        gather(d2_w[:], dw, k2_l[:])
        gather(d1_w[:], dw, k1_l[:])
        ds2g = sbuf("ds2g", [P, S, PACK], F32, "staged")
        bias = sbuf("bias", [P, PACK], F32)
        nc.vector.scalar_tensor_tensor(bias[:], sl_t[:], -1.0, th_t[:], ALU.mult, ALU.mult)

        for t in range(TILES):
            if t == 0:
                scatter(ds[t], entries(n1_l, 0, HALF), y[t][:, 0:HALF])
                scatter(ds2[t], n2_l[:], y[t][:])
                scatter(ds[t], entries(n1_l, HALF, S), y[t][:, HALF:S])
            else:
                scatter(ds2[t], n2_l[:], y[t][:])
                scatter(ds[t], n1_l[:], y[t][:])
            nc.vector.tensor_scalar(ds2g[:, :, t], ds2[t][:, 0:S], gs_t[:, t : t + 1], None, ALU.mult)

        h_pieces = [(0, 0, HALF, 5), (0, HALF, S, 6), (1, 0, S, 7), (2, 0, S, 0), (3, 0, S, 1)]
        h_acc = []
        for t, a, b, bank in h_pieces:
            acc = psum.tile([P, b - a], F32, name="h_acc%d" % bank, tag="bank%d" % bank)
            cols = slice(t * P, (t + 1) * P)
            product(acc[:], d2_w[:, cols], code_s[:, H + t * P : H + (t + 1) * P], two_w[:, a:b], two_s[:, a:b], True)
            h_acc.append(acc)

        z_w = sbuf("z_w", [P, S], U32)
        z_s = sbuf("z_s", [P, S], U8)
        h2 = [sbuf("h2_%d" % t, [P, S], F32) for t in range(TILES)]

        def close(i):
            t, a, b, bank = h_pieces[i]
            cols = slice(t * P, (t + 1) * P)
            product(h_acc[i][:], d1_w[:, cols], code_s[:, cols], z_w[:, a:b], z_s[:, a:b], False)
            if i == 1:
                nc.scalar.activation(h2[t][:, a:b], h_acc[i][:], ACT.Copy, scale=0.0625)
            else:
                nc.vector.tensor_scalar(h2[t][:, a:b], h_acc[i][:], 0.0625, None, ALU.mult)

        for c, (a, b) in enumerate(Z_CHUNKS):
            zb = sbuf("zb%d" % c, [P, b - a, PACK], BF16)
            for t0 in (0, 2):
                sg = sbuf("sg%d_%d" % (c, t0), [P, 2, b - a], F32)
                for t in (t0, t0 + 1):
                    nc.scalar.activation(
                        sg[:, t - t0, :], ds[t][:].indirect(entries(n3_l, a, b)), ACT.Sigmoid,
                        bias=bias[:, t : t + 1], scale=sl_t[:, t : t + 1],
                    )
                nc.vector.tensor_tensor(
                    zb[:, :, t0 : t0 + 2], ds2g[:, a:b, t0 : t0 + 2], sg[:].rearrange("p t j -> p j t"), ALU.mult
                )
            nc.vector.quantize_mx(
                out=z_w[:, a:b].bitcast(FP8X4), scales=z_s[:, a:b], in_=zb[:].rearrange("p j t -> p (j t)")
            )
            if c == 0:
                close(0)
        for i in range(1, len(h_pieces)):
            close(i)

        pa = [sbuf("pa%d" % t, [P, W], F32) for t in range(TILES)]
        pb = [sbuf("pb%d" % t, [P, W], F32) for t in range(TILES)]
        ra = [sbuf("ra%d" % t, [P, W], F32) for t in range(TILES)]
        rb = [sbuf("rb%d" % t, [P, W], F32) for t in range(TILES)]
        far = [sbuf("far%d" % t, [P, S], F32) for t in range(TILES)]
        res = [sbuf("res%d" % t, [P, S], F32) for t in range(TILES)]

        def pair(t):
            fetch(pa[t][:], h2[t], n4_l[:])
            fetch(pb[t][:], h2[t], n5_l[:])
            nc.vector.tensor_tensor(ra[t][:], pa[t][:], pb[t][:], ALU.add)
            nc.vector.tensor_tensor(rb[t][:], pa[t][:], pb[t][:], ALU.subtract)

        def finish(t, a, b):
            fetch(far[t][:, a:b], ub[t], entries(n6_l, a, b))
            nc.vector.tensor_tensor(res[t][:, a:b], ub[t][:, a:b], far[t][:, a:b], ALU.max)
            nc.sync.dma_start(out[t * P : (t + 1) * P, a:b], res[t][:, a:b])

        def put_back(tiles):
            for t in tiles:
                scatter(ub[t], n4_l[:], ra[t][:])
            for t in tiles:
                scatter(ub[t], n5_l[:], rb[t][:])

        pair(0)
        pair(1)
        put_back((0, 1))
        pair(2)
        pair(3)
        finish(0, 0, S)
        finish(1, 0, S)
        put_back((2, 3))
        finish(2, 0, S)
        finish(3, 0, S - 64)
        finish(3, S - 64, S)
